import numpy as np
import ml_dtypes


def mxq(x, axis, fmt="e4m3"):
    dtype, down = {"e4m3": (ml_dtypes.float8_e4m3fn, 7), "e5m2": (ml_dtypes.float8_e5m2, 14)}[fmt]
    v = np.moveaxis(np.asarray(x, np.float32).astype(ml_dtypes.bfloat16).astype(np.float64), axis, -1)
    blocks = v.reshape(v.shape[:-1] + (-1, 32))
    amax = np.abs(blocks).max(-1, keepdims=True)
    byte = np.maximum(np.where(amax > 0, np.frexp(amax)[1] - 1 + 127, 0) - down, 1)
    scale = np.exp2(byte - 127.0)
    codes = (blocks / scale).astype(np.float32).astype(dtype).astype(np.float64)
    return np.moveaxis((codes * scale).reshape(v.shape), -1, axis)


WIDE = False


def mx_kscale(k):
    if not WIDE:
        return np.ones(k)
    levels = np.array([10, -10, 5, -5, 0])
    if k % 512:
        return np.exp2(np.random.permutation(np.resize(levels, k // 32))).repeat(32)
    a = np.empty((k // 512, 16))
    for p in range(k // 512):
        a[p, :8] = np.random.permutation(np.resize(levels, 8))
        for g in range(8):
            far = levels[np.abs(levels - a[p, g]) >= 10]
            a[p, g + 8] = far[np.random.randint(len(far))]
    return np.exp2(a.ravel()).repeat(32)


def f64(x):
    return np.asarray(x).astype(np.float64)


def striped(idx):
    return np.tile(np.asarray(idx).reshape(-1, 16).T, (8, 1)).astype(np.uint16)


def unstriped(offs):
    return offs[:16].T.reshape(-1).astype(np.int64)


def striped8(idx):
    return np.asarray(idx).reshape(8, -1, 16).transpose(0, 2, 1).reshape(128, -1).astype(np.uint16)


def unstriped8(offs):
    return offs.reshape(8, 16, -1).transpose(0, 2, 1).reshape(8, -1).astype(np.int64)


def pick8(x, idx, run):
    r = np.arange(len(x))
    return x[r[:, None], idx[r % (8 * run) // run]]


E2M1 = np.array([0.0, 0.5, 1.0, 1.5, 2.0, 3.0, 4.0, 6.0, -0.0, -0.5, -1.0, -1.5, -2.0, -3.0, -4.0, -6.0])


def pack_weight(w, fmt):
    k, n = w.shape
    w = f64(np.asarray(w, np.float32).astype(ml_dtypes.bfloat16)).reshape(k // 32, 32, n)
    amax = np.abs(w).max(1)
    if fmt == "e4m3":
        byte = np.frexp(amax)[1] - 1 + 127 - 7
    else:
        mant, ex = np.frexp(amax / 6.0)
        byte = np.where(mant > 0.5, ex, ex - 1) + 127
    byte = np.clip(np.where(amax > 0, byte, 1), 1, 254)
    scaled = (w * np.exp2(127.0 - byte)[:, None, :]).reshape(k, n).astype(np.float32)
    by_word = np.ascontiguousarray(scaled.reshape(k // 512, 128, 4, n).transpose(0, 1, 3, 2))
    if fmt == "e4m3":
        words = by_word.astype(ml_dtypes.float8_e4m3fn).view(np.uint8)
    else:
        c = by_word.astype(ml_dtypes.float4_e2m1fn).view(np.uint8) & 0xF
        words = (c[..., 0::2] | (c[..., 1::2] << 4)).reshape(k // 512, 128, 2 * n)
    return np.ascontiguousarray(words), np.ascontiguousarray(byte.astype(np.uint8).reshape(k // 512, 16, n))


def unpack_weight(words, scales, fmt):
    g, _, n = scales.shape
    words = np.ascontiguousarray(words).reshape(g, 128, n, -1)
    if fmt == "e4m3":
        vals = words.view(ml_dtypes.float8_e4m3fn).astype(np.float64)
    else:
        nib = np.empty((g, 128, n, 4), np.uint8)
        nib[..., 0::2] = words & 0xF
        nib[..., 1::2] = words >> 4
        vals = E2M1[nib]
    vals = vals * np.repeat(np.exp2(scales.astype(np.float64) - 127.0), 8, axis=1)[..., None]
    return vals.transpose(0, 1, 3, 2).reshape(g * 512, n)


def bf(x):
    return np.asarray(x, np.float32).astype(ml_dtypes.bfloat16)


def planes(Y):
    r, m = Y.shape
    b = f64(bf(Y)).reshape(r // 32, 32, m)
    amax = np.abs(b).max(1)
    byte = np.clip(np.where(amax > 0, np.frexp(amax)[1] - 1 + 127 - 7, 1), 1, 254)
    codes = (b * np.exp2(127.0 - byte)[:, None, :]).reshape(r, m).astype(np.float32).astype(ml_dtypes.float8_e4m3fn).view(np.uint8)
    words = codes.reshape(r // 512, 128, 4, m).transpose(0, 1, 3, 2)
    return np.ascontiguousarray(words), np.ascontiguousarray(byte.astype(np.uint8).reshape(r // 512, 16, m))


K, R, F, T, J, U = 512, 512, 512, 2048, 256, 512


def setup_inputs():
    n = np.random.standard_normal
    idx = np.random.permutation(T)[:J]
    idx2 = np.stack([np.random.permutation(U)[:J] for _ in range(8)])
    idx3 = np.stack([np.random.permutation(U)[:J] for _ in range(8)])
    fk = mx_kscale(K)
    fr = mx_kscale(R)
    dtabp = pack_weight(n((K, T)) / fk[:, None], "e4m3")
    tabp = pack_weight(n((K, T)) / fk[:, None], "e4m3")
    return {
        "dtab_words": dtabp[0],
        "dtab_scales": dtabp[1],
        "tab_words": tabp[0],
        "tab_scales": tabp[1],
        "w1": (n((K, R)) * 1 / np.sqrt(K) * fk[:, None]).astype(np.float32),
        "gain": (np.random.uniform(0.5, 1.5, (R, 1))).astype(np.float32),
        "ground": (n((R, U)) * 0.7).astype(np.float32),
        "rs": (np.random.uniform(0.5, 2.0, (R, 1)) * fr[:, None]).astype(np.float32),
        "wor": (n((R, F)) * 1 / np.sqrt(R) / fr[:, None]).astype(np.float32),
        "res": (n((F, U)) * 0.5).astype(np.float32),
        "offs": striped(idx),
        "offs2": striped8(idx2),
        "offs3": striped8(idx3),
    }


def reference(dtab_words, dtab_scales, tab_words, tab_scales, w1, gain, ground, rs, wor, res, offs, offs2, offs3):
    idx = unstriped(offs)
    idx2 = unstriped8(offs2)
    idx3 = unstriped8(offs3)
    dtabu = unpack_weight(dtab_words, dtab_scales, "e4m3")
    tabu = unpack_weight(tab_words, tab_scales, "e4m3")
    w1q = mxq(f64(w1), 0, "e4m3")
    tabidxg = tabu[:, idx]
    a = w1q.T @ tabidxg
    dtabidxg = dtabu[:, idx]
    ta = w1q.T @ dtabidxg
    h1 = a * f64(gain)
    pa = np.zeros((R, U))
    pa[np.arange(R)[:, None], idx2[np.arange(R) % 512 // 64]] = h1
    pb = np.zeros((R, U))
    pb[np.arange(R)[:, None], idx3[np.arange(R) % 512 // 64]] = a
    th1 = ta * f64(gain)
    tpa = np.zeros((R, U))
    tpa[np.arange(R)[:, None], idx2[np.arange(R) % 512 // 64]] = th1
    tpb = np.zeros((R, U))
    tpb[np.arange(R)[:, None], idx3[np.arange(R) % 512 // 64]] = ta
    tu1 = tpa * (1.0 - np.square(np.tanh(pa + f64(ground)))) * (pb + f64(ground)) + tpb * np.tanh(pa + f64(ground))
    fo1 = tu1 * f64(rs)
    worq = mxq(f64(wor), 0, "e4m3")
    fo1q = mxq(fo1, 0, "e4m3")
    yo = worq.T @ fo1q
    y = yo + f64(res)
    words, scales = planes(y)
    return y, words, scales

@@ -1,0 +1,175 @@
+from contextlib import ExitStack
+
+import concourse.mybir as mybir
+
+F32 = mybir.dt.float32
+BF16 = mybir.dt.bfloat16
+I32 = mybir.dt.int32
+U32 = mybir.dt.uint32
+U16 = mybir.dt.uint16
+U8 = mybir.dt.uint8
+FP8X4 = mybir.dt.float8_e4m3fn_x4
+ACT = mybir.ActivationFunctionType
+ALU = mybir.AluOpType
+
+P = 128
+PACK = 4
+K, R, F, T, J, U = 512, 512, 512, 2048, 256, 512
+CH = 128
+VEC_COLS = 80
+
+FLOPS = 2 * K * R * J * 2 + 2 * R * F * U
+
+
+def tile_attend_ttwopages_o_pl_kernel(tc, dtab_words, dtab_scales, tab_words, tab_scales, w1, gain, ground, rs, wor, res,
+                                       offs, offs2, offs3, out_0, out_1, out_2):
+    nc = tc.nc
+    with ExitStack() as ctx:
+        lists = ctx.enter_context(tc.tile_pool(name="lists", bufs=1))
+        keep = ctx.enter_context(tc.tile_pool(name="keep", bufs=1))
+        psum = ctx.enter_context(tc.psum_pool(name="psum", bufs=1))
+
+        def zeroed(shape, dtype, name):
+            tile = keep.tile(shape, dtype, name=name, align_bytes=64)
+            nc.vector.memset(tile[:].bitcast(I32), 0)
+            return tile
+
+        def load(queue, shape, dtype, name, src, pool=keep):
+            tile = pool.tile(shape, dtype, name=name)
+            queue.dma_start(tile[:], src)
+            return tile
+
+        def load_scale_rows(queue, plane, scales):
+            for q in range(4):
+                queue.dma_start(plane[32 * q:32 * q + 4, :].bitcast(I32), scales[0, 4 * q:4 * q + 4, :].bitcast(I32))
+
+        def words_of(ap):
+            return ap[0].rearrange("p n t -> p (n t)").bitcast(I32)
+
+        def by_place(ap):
+            return ap.rearrange("(p t) n -> p t n", t=PACK)
+
+        tab_plane = zeroed([P, T], U8, "tab_plane")
+        dtab_plane = zeroed([P, T], U8, "dtab_plane")
+        page_a = [zeroed([P, U], F32, "page_a%d" % t) for t in range(PACK)]
+        page_b = [zeroed([P, U], F32, "page_b%d" % t) for t in range(PACK)]
+
+        w1_raw = load(nc.sync, [P, PACK, R], F32, "w1_raw", by_place(w1))
+        cols = load(nc.sync, [P, J // 16], U16, "cols", offs, lists)
+        load_scale_rows(nc.scalar, tab_plane, tab_scales)
+        tab_sb = load(nc.sync, [P, T], I32, "tab_sb", words_of(tab_words))
+        gain_sb = load(nc.sync, [P, PACK], F32, "gain_sb", gain.rearrange("(p t) o -> p (t o)", t=PACK))
+        places_a = load(nc.sync, [P, J // 16], U16, "places_a", offs2, lists)
+        places_b = load(nc.sync, [P, J // 16], U16, "places_b", offs3, lists)
+        load_scale_rows(nc.sync, dtab_plane, dtab_scales)
+        dtab_sb = load(nc.sync, [P, T], I32, "dtab_sb", words_of(dtab_words))
+        ground_sb = [load(nc.sync, [P, U], F32, "ground%d" % t, by_place(ground)[:, t, :]) for t in range(PACK)]
+        rs_sb = load(nc.sync, [P, PACK], F32, "rs_sb", rs.rearrange("(p t) o -> p (t o)", t=PACK))
+        wor_raw = load(nc.sync, [P, PACK, F], F32, "wor_raw", by_place(wor))
+        res_sb = load(nc.sync, [P, PACK, U], F32, "res_sb", by_place(res))
+
+        def deal(copy, grouped, raw, m0, m1):
+            copy(grouped[:, :, m0:m1, :].rearrange("p t m j -> p m t j"),
+                 raw[:].rearrange("p j (m t) -> p m t j", t=PACK)[:, m0:m1, :, :])
+
+        def gather(words, plane, name):
+            codes = keep.tile([P, J], U32, name=name + "_codes", align_bytes=64)
+            scales = keep.tile([P, J], U8, name=name + "_scales", align_bytes=64)
+            nc.vector.tensor_copy(scales[:], plane[:].indirect(cols[:]))
+            nc.vector.tensor_copy(codes[:], words[:].bitcast(U32).indirect(cols[:]))
+            return codes, scales
+
+        w1_grouped = keep.tile([P, PACK, P, PACK], BF16, align_bytes=64)
+        deal(nc.vector.tensor_copy, w1_grouped, w1_raw, 0, VEC_COLS)
+        deal(nc.scalar.copy, w1_grouped, w1_raw, VEC_COLS, P)
+        w1_codes = keep.tile([P, R], U32, align_bytes=64)
+        w1_scales = keep.tile([P, R], U8, align_bytes=64)
+        for t in range(PACK):
+            nc.vector.quantize_mx(out=w1_codes[:, t * P:(t + 1) * P].bitcast(FP8X4), scales=w1_scales[:, t * P:(t + 1) * P],
+                                  in_=w1_grouped[:, t, :, :].rearrange("p m j -> p (m j)"))
+        tab_codes, tab_sc = gather(tab_sb, tab_plane, "tab")
+
+        first = [psum.tile([P, 2, J], F32, name="first%d" % t) for t in range(PACK)]
+
+        def first_layer(t, side, codes, scales):
+            nc.tensor.matmul_mx(out=first[t][:, side, :], lhsT=w1_codes[:, t * P:(t + 1) * P].bitcast(FP8X4),
+                                lhsT_scale=w1_scales[:, t * P:(t + 1) * P], rhs=codes[:].bitcast(FP8X4), rhs_scale=scales[:],
+                                start=True, stop=True)
+
+        def put_on_pages(t, side, staged):
+            nc.scalar.activation(staged[:, 0:J], first[t][:, side, :], ACT.Copy, scale=gain_sb[:, t:t + 1])
+            nc.scalar.copy(staged[:, J:2 * J], first[t][:, side, :])
+            nc.vector.tensor_copy(page_a[t][:].indirect(places_a[:]), staged[:, 0:J])
+            nc.vector.tensor_copy(page_b[t][:].indirect(places_b[:]), staged[:, J:2 * J])
+
+        for t in range(PACK):
+            first_layer(t, 0, tab_codes, tab_sc)
+            staged = keep.tile([P, 2 * J], F32, name="staged%d" % t)
+            put_on_pages(t, 0, staged)
+
+        dtab_codes, dtab_sc = gather(dtab_sb, dtab_plane, "dtab")
+        for t in range(PACK):
+            first_layer(t, 1, dtab_codes, dtab_sc)
+
+        z, th, slope = [], [], []
+        for t in range(PACK):
+            z.append(keep.tile([P, U], F32, name="z%d" % t))
+            th.append(keep.tile([P, U], F32, name="th%d" % t))
+            slope.append(keep.tile([P, U], F32, name="slope%d" % t))
+            sq = keep.tile([P, U], F32, name="sq%d" % t)
+            w = keep.tile([P, U], F32, name="w%d" % t)
+            nc.gpsimd.tensor_tensor(z[t][:], page_a[t][:], ground_sb[t][:], ALU.add)
+            nc.scalar.activation(th[t][:], z[t][:], ACT.Tanh)
+            nc.scalar.activation(sq[:], th[t][:], ACT.Square)
+            nc.scalar.activation(sq[:], sq[:], ACT.Copy, scale=-1.0, bias=1.0)
+            nc.gpsimd.tensor_tensor(w[:], page_b[t][:], ground_sb[t][:], ALU.add)
+            nc.gpsimd.tensor_tensor(slope[t][:], sq[:], w[:], ALU.mult)
+
+        wor_grouped = keep.tile([P, PACK, P, PACK], BF16, align_bytes=64)
+        for m0 in range(0, P, 32):
+            deal(nc.scalar.copy, wor_grouped, wor_raw, m0, m0 + 32)
+        wor_codes = keep.tile([P, F], U32, align_bytes=64)
+        wor_scales = keep.tile([P, F], U8, align_bytes=64)
+        nc.vector.quantize_mx(out=wor_codes[:].bitcast(FP8X4), scales=wor_scales[:],
+                              in_=wor_grouped[:].rearrange("p t m j -> p (t m j)"))
+
+        fo_grouped = keep.tile([P, U, PACK], BF16, align_bytes=64)
+        last = PACK - 1
+        for t in range(PACK):
+            put_on_pages(t, 1, z[t])
+            nc.gpsimd.tensor_tensor(slope[t][:], page_a[t][:], slope[t][:], ALU.mult)
+            if t < last:
+                nc.gpsimd.tensor_tensor(th[t][:], page_b[t][:], th[t][:], ALU.mult)
+                nc.gpsimd.tensor_tensor(th[t][:], th[t][:], slope[t][:], ALU.add)
+                nc.scalar.activation(fo_grouped[:, :, t], th[t][:], ACT.Copy, scale=rs_sb[:, t:t + 1])
+
+        fo_codes = keep.tile([P, U], U32, align_bytes=64)
+        fo_scales = keep.tile([P, U], U8, align_bytes=64)
+        y_codes = keep.tile([P, U], U32, align_bytes=64)
+        y_scales = keep.tile([P, U], U8, align_bytes=64)
+        y_grouped = keep.tile([P, U, PACK], BF16, align_bytes=64)
+        chunks = [slice(u0, u0 + CH) for u0 in range(0, U, CH)]
+        for us in chunks:
+            nc.vector.tensor_tensor(th[last][:, us], page_b[last][:, us], th[last][:, us], ALU.mult)
+        for us in chunks:
+            nc.vector.tensor_tensor(th[last][:, us], th[last][:, us], slope[last][:, us], ALU.add)
+            nc.scalar.activation(fo_grouped[:, us, last], th[last][:, us], ACT.Copy, scale=rs_sb[:, last:last + 1])
+        for c, us in enumerate(chunks):
+            nc.vector.quantize_mx(out=fo_codes[:, us].bitcast(FP8X4), scales=fo_scales[:, us],
+                                  in_=fo_grouped[:, us, :].rearrange("p u j -> p (u j)"))
+            second = psum.tile([P, PACK, CH], F32, name="second%d" % c)
+            for t in range(PACK):
+                nc.tensor.matmul_mx(out=second[:, t, :], lhsT=wor_codes[:, t * P:(t + 1) * P].bitcast(FP8X4),
+                                    lhsT_scale=wor_scales[:, t * P:(t + 1) * P], rhs=fo_codes[:, us].bitcast(FP8X4),
+                                    rhs_scale=fo_scales[:, us], start=True, stop=True)
+            y = keep.tile([P, PACK, CH], F32, name="y%d" % c)
+            nc.vector.tensor_tensor(y[:], second[:], res_sb[:, :, us], ALU.add)
+            nc.sync.dma_start(by_place(out_0)[:, :, us], y[:])
+            nc.scalar.copy(y_grouped[:, us, :].rearrange("p (c i) t -> p c t i", i=4),
+                           y[:].rearrange("p t (c i) -> p c t i", i=4))
+            nc.vector.quantize_mx(out=y_codes[:, us].bitcast(FP8X4), scales=y_scales[:, us],
+                                  in_=y_grouped[:, us, :].rearrange("p u j -> p (u j)"))
+            nc.sync.dma_start(words_of(out_1)[:, us], y_codes[:, us].bitcast(I32))
+        for q in range(4):
+            queue = nc.scalar if q % 2 else nc.sync
+            queue.dma_start(out_2[0, 4 * q:4 * q + 4, :].bitcast(I32), y_scales[32 * q:32 * q + 4, :].bitcast(I32))

@@ -1,6 +1,7 @@
 from contextlib import ExitStack
 
 import concourse.mybir as mybir
+from concourse.masks import make_identity
 
 F32 = mybir.dt.float32
 BF16 = mybir.dt.bfloat16
@@ -13,12 +14,14 @@ ACT = mybir.ActivationFunctionType
 ALU = mybir.AluOpType
 
 P = 128
-PACK = 4
+PLACES = 4
+QUADRANTS = 4
 K, R, F, T, J, U = 512, 512, 512, 2048, 256, 512
-CH = 128
-VEC_COLS = 80
+LAST = PLACES - 1
+W1_ON_VECTOR = 72
+WOR_PIECE = 32
 
-FLOPS = 2 * K * R * J * 2 + 2 * R * F * U
+FLOPS = 2 * (2 * K * R * J) + 2 * R * F * U
 
 
 def tile_attend_ttwopages_o_pl_kernel(tc, dtab_words, dtab_scales, tab_words, tab_scales, w1, gain, ground, rs, wor, res,
@@ -27,149 +30,192 @@ def tile_attend_ttwopages_o_pl_kernel(tc, dtab_words, dtab_scales, tab_words, ta
     with ExitStack() as ctx:
         lists = ctx.enter_context(tc.tile_pool(name="lists", bufs=1))
         keep = ctx.enter_context(tc.tile_pool(name="keep", bufs=1))
+        turn = ctx.enter_context(tc.psum_pool(name="turn", bufs=1))
         psum = ctx.enter_context(tc.psum_pool(name="psum", bufs=1))
 
-        def zeroed(shape, dtype, name):
+        def zeroed(shape, dtype, name, engine=nc.vector):
             tile = keep.tile(shape, dtype, name=name, align_bytes=64)
-            nc.vector.memset(tile[:].bitcast(I32), 0)
+            engine.memset(tile[:].bitcast(I32), 0)
             return tile
 
-        def load(queue, shape, dtype, name, src, pool=keep):
-            tile = pool.tile(shape, dtype, name=name)
-            queue.dma_start(tile[:], src)
+        def load(shape, dtype, name, src, pool=keep):
+            tile = pool.tile(shape, dtype, name=name, align_bytes=64)
+            nc.sync.dma_start(tile[:], src)
             return tile
 
-        def load_scale_rows(queue, plane, scales):
-            for q in range(4):
-                queue.dma_start(plane[32 * q:32 * q + 4, :].bitcast(I32), scales[0, 4 * q:4 * q + 4, :].bitcast(I32))
+        def load_scale_rows(scales, name):
+            rows = keep.tile([P, T], U8, name=name, align_bytes=64)
+            nc.scalar.dma_start(rows[0:32, :].bitcast(I32), scales[0].bitcast(I32).unsqueeze(1).broadcast_to([16, 2, T // 4]))
+            nc.vector.memset(rows[32:64, :].bitcast(I32), 0)
+            nc.vector.memset(rows[64:P, :].bitcast(I32), 0)
+            return rows
 
         def words_of(ap):
             return ap[0].rearrange("p n t -> p (n t)").bitcast(I32)
 
         def by_place(ap):
-            return ap.rearrange("(p t) n -> p t n", t=PACK)
+            return ap.rearrange("(p t) n -> p t n", t=PLACES)
 
-        tab_plane = zeroed([P, T], U8, "tab_plane")
-        dtab_plane = zeroed([P, T], U8, "dtab_plane")
-        page_a = [zeroed([P, U], F32, "page_a%d" % t) for t in range(PACK)]
-        page_b = [zeroed([P, U], F32, "page_b%d" % t) for t in range(PACK)]
+        def by_column(ap):
+            return ap.rearrange("p t u -> p u t")
 
-        w1_raw = load(nc.sync, [P, PACK, R], F32, "w1_raw", by_place(w1))
-        cols = load(nc.sync, [P, J // 16], U16, "cols", offs, lists)
-        load_scale_rows(nc.scalar, tab_plane, tab_scales)
-        tab_sb = load(nc.sync, [P, T], I32, "tab_sb", words_of(tab_words))
-        gain_sb = load(nc.sync, [P, PACK], F32, "gain_sb", gain.rearrange("(p t) o -> p (t o)", t=PACK))
-        places_a = load(nc.sync, [P, J // 16], U16, "places_a", offs2, lists)
-        places_b = load(nc.sync, [P, J // 16], U16, "places_b", offs3, lists)
-        load_scale_rows(nc.sync, dtab_plane, dtab_scales)
-        dtab_sb = load(nc.sync, [P, T], I32, "dtab_sb", words_of(dtab_words))
-        ground_sb = [load(nc.sync, [P, U], F32, "ground%d" % t, by_place(ground)[:, t, :]) for t in range(PACK)]
-        rs_sb = load(nc.sync, [P, PACK], F32, "rs_sb", rs.rearrange("(p t) o -> p (t o)", t=PACK))
-        wor_raw = load(nc.sync, [P, PACK, F], F32, "wor_raw", by_place(wor))
-        res_sb = load(nc.sync, [P, PACK, U], F32, "res_sb", by_place(res))
+        ident = keep.tile([P, P], F32)
+        make_identity(nc, ident[:])
+        tab_rows = load_scale_rows(tab_scales, "tab_rows")
+        dtab_rows = load_scale_rows(dtab_scales, "dtab_rows")
+        listed_scales = zeroed([P, 2 * J], U8, "listed_scales")
 
-        def deal(copy, grouped, raw, m0, m1):
-            copy(grouped[:, :, m0:m1, :].rearrange("p t m j -> p m t j"),
-                 raw[:].rearrange("p j (m t) -> p m t j", t=PACK)[:, m0:m1, :, :])
+        columns = load([P, J // 16], U16, "columns", offs, lists)
+        w1_raw = load([P, PLACES, R], F32, "w1_raw", by_place(w1))
+        tab_sb = load([P, T], I32, "tab_sb", words_of(tab_words))
 
-        def gather(words, plane, name):
-            codes = keep.tile([P, J], U32, name=name + "_codes", align_bytes=64)
-            scales = keep.tile([P, J], U8, name=name + "_scales", align_bytes=64)
-            nc.vector.tensor_copy(scales[:], plane[:].indirect(cols[:]))
-            nc.vector.tensor_copy(codes[:], words[:].bitcast(U32).indirect(cols[:]))
-            return codes, scales
+        picked = keep.tile([P, 2 * J], U8, align_bytes=64)
+        nc.vector.tensor_copy(picked[:, 0:J], tab_rows[:].indirect(columns[:]))
+        nc.vector.tensor_copy(picked[:, J:2 * J], dtab_rows[:].indirect(columns[:]))
+        for q in range(QUADRANTS):
+            nc.sync.dma_start(listed_scales[32 * q:32 * q + 4, :].bitcast(I32), picked[8 * q:8 * q + 8:2, :].bitcast(I32))
 
-        w1_grouped = keep.tile([P, PACK, P, PACK], BF16, align_bytes=64)
-        deal(nc.vector.tensor_copy, w1_grouped, w1_raw, 0, VEC_COLS)
-        deal(nc.scalar.copy, w1_grouped, w1_raw, VEC_COLS, P)
+        dtab_sb = load([P, T], I32, "dtab_sb", words_of(dtab_words))
+        slots_a = load([P, J // 16], U16, "slots_a", offs2, lists)
+        gain_sb = load([P, PLACES], F32, "gain_sb", gain.rearrange("(p t) o -> p (t o)", t=PLACES))
+        rs_sb = load([P, PLACES], F32, "rs_sb", rs.rearrange("(p t) o -> p (t o)", t=PLACES))
+        slots_b = load([P, J // 16], U16, "slots_b", offs3, lists)
+        ground_sb = [load([P, U], F32, "ground%d" % t, by_place(ground)[:, t, :]) for t in range(PLACES)]
+        wor_raw = load([P, PLACES, F], F32, "wor_raw", by_place(wor))
+        res_sb = load([P, PLACES, U], F32, "res_sb", by_place(res))
+
+        def deal(copy, dealt, raw, m0, m1):
+            copy(dealt[:, :, m0:m1, :].rearrange("p t m j -> p m t j"),
+                 raw[:].rearrange("p j (m t) -> p m t j", t=PLACES)[:, m0:m1, :, :])
+
+        def gather_words(words, name):
+            codes = keep.tile([P, J], U32, name=name, align_bytes=64)
+            nc.vector.tensor_copy(codes[:], words[:].bitcast(U32).indirect(columns[:]))
+            return codes
+
+        blocks = [slice(c0, c0 + P) for c0 in range(0, U, P)]
+
+        w1_dealt = keep.tile([P, PLACES, P, PLACES], BF16, align_bytes=64)
+        deal(nc.vector.tensor_copy, w1_dealt, w1_raw, 0, W1_ON_VECTOR)
+        deal(nc.scalar.copy, w1_dealt, w1_raw, W1_ON_VECTOR, P)
         w1_codes = keep.tile([P, R], U32, align_bytes=64)
         w1_scales = keep.tile([P, R], U8, align_bytes=64)
-        for t in range(PACK):
-            nc.vector.quantize_mx(out=w1_codes[:, t * P:(t + 1) * P].bitcast(FP8X4), scales=w1_scales[:, t * P:(t + 1) * P],
-                                  in_=w1_grouped[:, t, :, :].rearrange("p m j -> p (m j)"))
-        tab_codes, tab_sc = gather(tab_sb, tab_plane, "tab")
+        for t in range(PLACES):
+            nc.vector.quantize_mx(out=w1_codes[:, blocks[t]].bitcast(FP8X4), scales=w1_scales[:, blocks[t]],
+                                  in_=w1_dealt[:, t, :, :].rearrange("p m j -> p (m j)"))
+        tab_codes = gather_words(tab_sb, "tab_codes")
 
-        first = [psum.tile([P, 2, J], F32, name="first%d" % t) for t in range(PACK)]
+        page_a = [zeroed([P, U], F32, name) for name in ("dtab_rows", "w1_raw", "page_a2", "w1_dealt")]
+        page_b = [zeroed([P, U], F32, "tab_rows", nc.gpsimd)]
+        page_b.extend(zeroed([P, U], F32, name) for name in ("picked", "page_b2", "tab_sb"))
 
-        def first_layer(t, side, codes, scales):
-            nc.tensor.matmul_mx(out=first[t][:, side, :], lhsT=w1_codes[:, t * P:(t + 1) * P].bitcast(FP8X4),
-                                lhsT_scale=w1_scales[:, t * P:(t + 1) * P], rhs=codes[:].bitcast(FP8X4), rhs_scale=scales[:],
-                                start=True, stop=True)
+        def first_layer(t, codes, scales, name):
+            bank = psum.tile([P, J], F32, name="first_bank")
+            nc.tensor.matmul_mx(out=bank[:], lhsT=w1_codes[:, blocks[t]].bitcast(FP8X4), lhsT_scale=w1_scales[:, blocks[t]],
+                                rhs=codes[:].bitcast(FP8X4), rhs_scale=scales, start=True, stop=True)
+            staged = keep.tile([P, 2, J], F32, name=name, align_bytes=64)
+            nc.scalar.activation(staged[:, 0, :], bank[:], ACT.Copy, scale=gain_sb[:, t:t + 1])
+            nc.scalar.copy(staged[:, 1, :], bank[:])
+            return staged
 
-        def put_on_pages(t, side, staged):
-            nc.scalar.activation(staged[:, 0:J], first[t][:, side, :], ACT.Copy, scale=gain_sb[:, t:t + 1])
-            nc.scalar.copy(staged[:, J:2 * J], first[t][:, side, :])
-            nc.vector.tensor_copy(page_a[t][:].indirect(places_a[:]), staged[:, 0:J])
-            nc.vector.tensor_copy(page_b[t][:].indirect(places_b[:]), staged[:, J:2 * J])
+        def put_on_pages(t, staged):
+            nc.vector.tensor_copy(page_a[t][:].indirect(slots_a[:]), staged[:, 0, :])
+            nc.vector.tensor_copy(page_b[t][:].indirect(slots_b[:]), staged[:, 1, :])
 
-        for t in range(PACK):
-            first_layer(t, 0, tab_codes, tab_sc)
-            staged = keep.tile([P, 2 * J], F32, name="staged%d" % t)
-            put_on_pages(t, 0, staged)
+        def turned_sum(x, y):
+            bank = turn.tile([P, U], F32, name="sum_bank")
+            for us in blocks:
+                nc.tensor.matmul(bank[:, us], lhsT=x[:, us], rhs=ident[:], is_transpose=True, start=True, stop=False)
+                nc.tensor.matmul(bank[:, us], lhsT=y[:, us], rhs=ident[:], is_transpose=True, start=False, stop=True)
+            return bank
 
-        dtab_codes, dtab_sc = gather(dtab_sb, dtab_plane, "dtab")
-        for t in range(PACK):
-            first_layer(t, 1, dtab_codes, dtab_sc)
+        def back_bank(shape):
+            return turn.tile(shape, F32, name="back_bank", bufs=3)
 
-        z, th, slope = [], [], []
-        for t in range(PACK):
-            z.append(keep.tile([P, U], F32, name="z%d" % t))
-            th.append(keep.tile([P, U], F32, name="th%d" % t))
-            slope.append(keep.tile([P, U], F32, name="slope%d" % t))
-            sq = keep.tile([P, U], F32, name="sq%d" % t)
-            w = keep.tile([P, U], F32, name="w%d" % t)
-            nc.gpsimd.tensor_tensor(z[t][:], page_a[t][:], ground_sb[t][:], ALU.add)
-            nc.scalar.activation(th[t][:], z[t][:], ACT.Tanh)
-            nc.scalar.activation(sq[:], th[t][:], ACT.Square)
-            nc.scalar.activation(sq[:], sq[:], ACT.Copy, scale=-1.0, bias=1.0)
-            nc.gpsimd.tensor_tensor(w[:], page_b[t][:], ground_sb[t][:], ALU.add)
-            nc.gpsimd.tensor_tensor(slope[t][:], sq[:], w[:], ALU.mult)
+        for t in range(PLACES):
+            put_on_pages(t, first_layer(t, tab_codes, listed_scales[:, 0:J], "forward%d" % t))
+        dtab_codes = gather_words(dtab_sb, "dtab_codes")
 
-        wor_grouped = keep.tile([P, PACK, P, PACK], BF16, align_bytes=64)
-        for m0 in range(0, P, 32):
-            deal(nc.scalar.copy, wor_grouped, wor_raw, m0, m0 + 32)
-        wor_codes = keep.tile([P, F], U32, align_bytes=64)
+        scaled_tanh = keep.tile([P, PLACES, U], F32)
+        second_factor = keep.tile([P, 2, U], F32)
+        slope = keep.tile([P, PLACES, U], F32)
+        neg_rs = keep.tile([P, PLACES], F32)
+        nc.scalar.activation(neg_rs[:], rs_sb[:], ACT.Copy, scale=-1.0)
+        damping = []
+        for t in range(PLACES):
+            tanh_turned = keep.tile([P, U], F32, name="tanh_turned%d" % t, align_bytes=64)
+            nc.scalar.activation(tanh_turned[:], turned_sum(ground_sb[t], page_a[t])[:], ACT.Tanh)
+            tanh_bank = back_bank([P, U])
+            for us in blocks:
+                nc.tensor.transpose(tanh_bank[:, us], tanh_turned[:, us], ident[:])
+            damping.append(keep.tile([P, U], F32, name="damping%d" % t, align_bytes=64))
+            nc.scalar.activation(damping[t][:], tanh_bank[:], ACT.Square)
+            nc.scalar.activation(damping[t][:], damping[t][:], ACT.Identity, scale=neg_rs[:, t:t + 1], bias=rs_sb[:, t:t + 1])
+            if t < LAST:
+                nc.scalar.activation(scaled_tanh[:, t, :], tanh_bank[:], ACT.Copy, scale=rs_sb[:, t:t + 1])
+            nc.gpsimd.tensor_tensor(second_factor[:, t % 2, :], page_b[t][:], ground_sb[t][:], ALU.add)
+            nc.gpsimd.tensor_tensor(slope[:, t, :], second_factor[:, t % 2, :], damping[t][:], ALU.mult)
+
+        tangents = [first_layer(t, dtab_codes, listed_scales[:, J:2 * J], "tangent%d" % t) for t in range(PLACES)]
+
+        wor_dealt = keep.tile([P, PLACES, P, PLACES], BF16, name="tanh_turned%d" % LAST, align_bytes=64)
+        for m0 in range(0, P, WOR_PIECE):
+            deal(nc.scalar.copy, wor_dealt, wor_raw, m0, m0 + WOR_PIECE)
+
+        term_a = [second_factor[:, 0, :]] + [slope[:, t, :] for t in range(LAST)]
+        term_b = [damping[2][:], scaled_tanh[:, 0, :], scaled_tanh[:, 1, :]]
+        fo_turned = [damping[0][:], scaled_tanh[:, LAST, :]]
+        for t in range(PLACES):
+            put_on_pages(t, tangents[t])
+            nc.gpsimd.tensor_tensor(term_a[t], page_a[t][:], slope[:, t, :], ALU.mult)
+            if t < LAST:
+                nc.gpsimd.tensor_tensor(term_b[t], page_b[t][:], scaled_tanh[:, t, :], ALU.mult)
+            if t < len(fo_turned):
+                nc.scalar.copy(fo_turned[t], turned_sum(term_a[t], term_b[t])[:])
+
+        pairs = [keep.tile([P, 2, P, 2], BF16, name="pairs%d" % c) for c in range(len(blocks))]
+        for half in range(2):
+            both = back_bank([P, 2, U // 2])
+            for b in range(2):
+                for t in (1, 0):
+                    nc.tensor.transpose(both[:, t, blocks[b]], fo_turned[t][:, blocks[2 * half + b]], ident[:])
+            for b in range(2):
+                nc.scalar.copy(pairs[2 * half + b][:, 0, :, :], by_column(both[:, :, blocks[b]]))
+
+        nc.vector.scalar_tensor_tensor(scaled_tanh[:, LAST, :], page_b[LAST][:], rs_sb[:, LAST:LAST + 1], tanh_bank[:],
+                                       ALU.mult, ALU.mult)
+        wor_codes = keep.tile([P, F], U32, name="damping0", align_bytes=64)
         wor_scales = keep.tile([P, F], U8, align_bytes=64)
         nc.vector.quantize_mx(out=wor_codes[:].bitcast(FP8X4), scales=wor_scales[:],
-                              in_=wor_grouped[:].rearrange("p t m j -> p (t m j)"))
-
-        fo_grouped = keep.tile([P, U, PACK], BF16, align_bytes=64)
-        last = PACK - 1
-        for t in range(PACK):
-            put_on_pages(t, 1, z[t])
-            nc.gpsimd.tensor_tensor(slope[t][:], page_a[t][:], slope[t][:], ALU.mult)
-            if t < last:
-                nc.gpsimd.tensor_tensor(th[t][:], page_b[t][:], th[t][:], ALU.mult)
-                nc.gpsimd.tensor_tensor(th[t][:], th[t][:], slope[t][:], ALU.add)
-                nc.scalar.activation(fo_grouped[:, :, t], th[t][:], ACT.Copy, scale=rs_sb[:, t:t + 1])
+                              in_=wor_dealt[:].rearrange("p t m j -> p (t m j)"))
 
         fo_codes = keep.tile([P, U], U32, align_bytes=64)
         fo_scales = keep.tile([P, U], U8, align_bytes=64)
         y_codes = keep.tile([P, U], U32, align_bytes=64)
         y_scales = keep.tile([P, U], U8, align_bytes=64)
-        y_grouped = keep.tile([P, U, PACK], BF16, align_bytes=64)
-        chunks = [slice(u0, u0 + CH) for u0 in range(0, U, CH)]
-        for us in chunks:
-            nc.vector.tensor_tensor(th[last][:, us], page_b[last][:, us], th[last][:, us], ALU.mult)
-        for us in chunks:
-            nc.vector.tensor_tensor(th[last][:, us], th[last][:, us], slope[last][:, us], ALU.add)
-            nc.scalar.activation(fo_grouped[:, us, last], th[last][:, us], ACT.Copy, scale=rs_sb[:, last:last + 1])
-        for c, us in enumerate(chunks):
-            nc.vector.quantize_mx(out=fo_codes[:, us].bitcast(FP8X4), scales=fo_scales[:, us],
-                                  in_=fo_grouped[:, us, :].rearrange("p u j -> p (u j)"))
-            second = psum.tile([P, PACK, CH], F32, name="second%d" % c)
-            for t in range(PACK):
-                nc.tensor.matmul_mx(out=second[:, t, :], lhsT=wor_codes[:, t * P:(t + 1) * P].bitcast(FP8X4),
-                                    lhsT_scale=wor_scales[:, t * P:(t + 1) * P], rhs=fo_codes[:, us].bitcast(FP8X4),
-                                    rhs_scale=fo_scales[:, us], start=True, stop=True)
-            y = keep.tile([P, PACK, CH], F32, name="y%d" % c)
-            nc.vector.tensor_tensor(y[:], second[:], res_sb[:, :, us], ALU.add)
+        y_rounded = keep.tile([P, U, PLACES], BF16, align_bytes=64)
+        for c, us in enumerate(blocks):
+            at_end = c == len(blocks) - 1
+            nc.vector.tensor_tensor(pairs[c][:, 1, :, :], by_column(slope[:, 1:3, us]), by_column(scaled_tanh[:, 1:4:2, us]),
+                                    ALU.add)
+            fo_rounded = keep.tile([P, PLACES * P], BF16, name="fo_rounded%d" % c, align_bytes=64)
+            nc.scalar.copy(fo_rounded[:].bitcast(F32).rearrange("p (u h) -> p u h", h=2),
+                           pairs[c][:].rearrange("p h u e -> p (h u e)").bitcast(F32).rearrange("p (h u) -> p u h", h=2))
+            nc.vector.quantize_mx(out=fo_codes[:, us].bitcast(FP8X4), scales=fo_scales[:, us], in_=fo_rounded[:])
+            yo = psum.tile([P, PLACES, P], F32, name="first_bank" if at_end else "last_bank%d" % c)
+            for t in range(PLACES):
+                nc.tensor.matmul_mx(out=yo[:, t, :], lhsT=wor_codes[:, blocks[t]].bitcast(FP8X4), lhsT_scale=wor_scales[:, blocks[t]],
+                                    rhs=fo_codes[:, us].bitcast(FP8X4), rhs_scale=fo_scales[:, us], start=True, stop=True)
+            y = keep.tile([P, PLACES, P], F32, name="y%d" % c)
+            nc.vector.tensor_tensor(y[:], yo[:], res_sb[:, :, us], ALU.add)
             nc.sync.dma_start(by_place(out_0)[:, :, us], y[:])
-            nc.scalar.copy(y_grouped[:, us, :].rearrange("p (c i) t -> p c t i", i=4),
-                           y[:].rearrange("p t (c i) -> p c t i", i=4))
+            copy = nc.vector.tensor_copy if at_end else nc.scalar.copy
+            copy(y_rounded[:, us, :].rearrange("p (g i) t -> p g t i", i=4), y[:].rearrange("p t (g i) -> p g t i", i=4))
             nc.vector.quantize_mx(out=y_codes[:, us].bitcast(FP8X4), scales=y_scales[:, us],
-                                  in_=y_grouped[:, us, :].rearrange("p u j -> p (u j)"))
+                                  in_=y_rounded[:, us, :].rearrange("p u t -> p (u t)"))
+
+        for us in (slice(0, U - P), blocks[-1]):
             nc.sync.dma_start(words_of(out_1)[:, us], y_codes[:, us].bitcast(I32))
-        for q in range(4):
+        for q in range(QUADRANTS):
             queue = nc.scalar if q % 2 else nc.sync
             queue.dma_start(out_2[0, 4 * q:4 * q + 4, :].bitcast(I32), y_scales[32 * q:32 * q + 4, :].bitcast(I32))

@@ -173,14 +173,13 @@ def tile_attend_ttwopages_o_pl_kernel(tc, dtab_words, dtab_scales, tab_words, ta
             if t < len(fo_turned):
                 nc.scalar.copy(fo_turned[t], turned_sum(term_a[t], term_b[t])[:])
 
-        pairs = [keep.tile([P, 2, P, 2], BF16, name="pairs%d" % c) for c in range(len(blocks))]
+        fo_rounded = keep.tile([P, U, PLACES], BF16, align_bytes=64)
         for half in range(2):
             both = back_bank([P, 2, U // 2])
             for b in range(2):
                 for t in (1, 0):
                     nc.tensor.transpose(both[:, t, blocks[b]], fo_turned[t][:, blocks[2 * half + b]], ident[:])
-            for b in range(2):
-                nc.scalar.copy(pairs[2 * half + b][:, 0, :, :], by_column(both[:, :, blocks[b]]))
+            nc.scalar.copy(fo_rounded[:, half * (U // 2):(half + 1) * (U // 2), 0:2], by_column(both[:]))
 
         nc.vector.scalar_tensor_tensor(scaled_tanh[:, LAST, :], page_b[LAST][:], rs_sb[:, LAST:LAST + 1], tanh_bank[:],
                                        ALU.mult, ALU.mult)
@@ -194,22 +193,22 @@ def tile_attend_ttwopages_o_pl_kernel(tc, dtab_words, dtab_scales, tab_words, ta
         y_codes = keep.tile([P, U], U32, align_bytes=64)
         y_scales = keep.tile([P, U], U8, align_bytes=64)
         y_rounded = keep.tile([P, U, PLACES], BF16, align_bytes=64)
+        products = []
         for c, us in enumerate(blocks):
-            at_end = c == len(blocks) - 1
-            nc.vector.tensor_tensor(pairs[c][:, 1, :, :], by_column(slope[:, 1:3, us]), by_column(scaled_tanh[:, 1:4:2, us]),
+            nc.vector.tensor_tensor(fo_rounded[:, us, 2:4], by_column(slope[:, 1:3, us]), by_column(scaled_tanh[:, 1:4:2, us]),
                                     ALU.add)
-            fo_rounded = keep.tile([P, PLACES * P], BF16, name="fo_rounded%d" % c, align_bytes=64)
-            nc.scalar.copy(fo_rounded[:].bitcast(F32).rearrange("p (u h) -> p u h", h=2),
-                           pairs[c][:].rearrange("p h u e -> p (h u e)").bitcast(F32).rearrange("p (h u) -> p u h", h=2))
-            nc.vector.quantize_mx(out=fo_codes[:, us].bitcast(FP8X4), scales=fo_scales[:, us], in_=fo_rounded[:])
-            yo = psum.tile([P, PLACES, P], F32, name="first_bank" if at_end else "last_bank%d" % c)
+            nc.vector.quantize_mx(out=fo_codes[:, us].bitcast(FP8X4), scales=fo_scales[:, us],
+                                  in_=fo_rounded[:, us, :].rearrange("p u t -> p (u t)"))
+            yo = psum.tile([P, PLACES, P], F32, name="first_bank" if c == len(blocks) - 1 else "last_bank%d" % c)
             for t in range(PLACES):
                 nc.tensor.matmul_mx(out=yo[:, t, :], lhsT=wor_codes[:, blocks[t]].bitcast(FP8X4), lhsT_scale=wor_scales[:, blocks[t]],
                                     rhs=fo_codes[:, us].bitcast(FP8X4), rhs_scale=fo_scales[:, us], start=True, stop=True)
+            products.append(yo)
+        for c, (us, yo) in enumerate(zip(blocks, products)):
             y = keep.tile([P, PLACES, P], F32, name="y%d" % c)
             nc.vector.tensor_tensor(y[:], yo[:], res_sb[:, :, us], ALU.add)
             nc.sync.dma_start(by_place(out_0)[:, :, us], y[:])
-            copy = nc.vector.tensor_copy if at_end else nc.scalar.copy
+            copy = nc.vector.tensor_copy if c == len(blocks) - 1 else nc.scalar.copy
             copy(y_rounded[:, us, :].rearrange("p (g i) t -> p g t i", i=4), y[:].rearrange("p t (g i) -> p g t i", i=4))
             nc.vector.quantize_mx(out=y_codes[:, us].bitcast(FP8X4), scales=y_scales[:, us],
                                   in_=y_rounded[:, us, :].rearrange("p u t -> p (u t)"))

from contextlib import ExitStack

import concourse.mybir as mybir
from concourse.masks import make_identity

F32 = mybir.dt.float32
BF16 = mybir.dt.bfloat16
I32 = mybir.dt.int32
U32 = mybir.dt.uint32
U16 = mybir.dt.uint16
U8 = mybir.dt.uint8
FP8X4 = mybir.dt.float8_e4m3fn_x4
ACT = mybir.ActivationFunctionType
ALU = mybir.AluOpType

P = 128
PLACES = 4
QUADRANTS = 4
K, R, F, T, J, U = 512, 512, 512, 2048, 256, 512
LAST = PLACES - 1
W1_ON_VECTOR = 72
WOR_PIECE = 32

FLOPS = 2 * (2 * K * R * J) + 2 * R * F * U


def tile_attend_ttwopages_o_pl_kernel(tc, dtab_words, dtab_scales, tab_words, tab_scales, w1, gain, ground, rs, wor, res,
                                       offs, offs2, offs3, out_0, out_1, out_2):
    nc = tc.nc
    with ExitStack() as ctx:
        lists = ctx.enter_context(tc.tile_pool(name="lists", bufs=1))
        keep = ctx.enter_context(tc.tile_pool(name="keep", bufs=1))
        turn = ctx.enter_context(tc.psum_pool(name="turn", bufs=1))
        psum = ctx.enter_context(tc.psum_pool(name="psum", bufs=1))

        def zeroed(shape, dtype, name, engine=nc.vector):
            tile = keep.tile(shape, dtype, name=name, align_bytes=64)
            engine.memset(tile[:].bitcast(I32), 0)
            return tile

        def load(shape, dtype, name, src, pool=keep):
            tile = pool.tile(shape, dtype, name=name, align_bytes=64)
            nc.sync.dma_start(tile[:], src)
            return tile

        def load_scale_rows(scales, name):
            rows = keep.tile([P, T], U8, name=name, align_bytes=64)
            nc.scalar.dma_start(rows[0:32, :].bitcast(I32), scales[0].bitcast(I32).unsqueeze(1).broadcast_to([16, 2, T // 4]))
            nc.vector.memset(rows[32:64, :].bitcast(I32), 0)
            nc.vector.memset(rows[64:P, :].bitcast(I32), 0)
            return rows

        def words_of(ap):
            return ap[0].rearrange("p n t -> p (n t)").bitcast(I32)

        def by_place(ap):
            return ap.rearrange("(p t) n -> p t n", t=PLACES)

        def by_column(ap):
            return ap.rearrange("p t u -> p u t")

        ident = keep.tile([P, P], F32)
        make_identity(nc, ident[:])
        tab_rows = load_scale_rows(tab_scales, "tab_rows")
        dtab_rows = load_scale_rows(dtab_scales, "dtab_rows")
        listed_scales = zeroed([P, 2 * J], U8, "listed_scales")

        columns = load([P, J // 16], U16, "columns", offs, lists)
        w1_raw = load([P, PLACES, R], F32, "w1_raw", by_place(w1))
        tab_sb = load([P, T], I32, "tab_sb", words_of(tab_words))

        picked = keep.tile([P, 2 * J], U8, align_bytes=64)
        nc.vector.tensor_copy(picked[:, 0:J], tab_rows[:].indirect(columns[:]))
        nc.vector.tensor_copy(picked[:, J:2 * J], dtab_rows[:].indirect(columns[:]))
        for q in range(QUADRANTS):
            nc.sync.dma_start(listed_scales[32 * q:32 * q + 4, :].bitcast(I32), picked[8 * q:8 * q + 8:2, :].bitcast(I32))

        dtab_sb = load([P, T], I32, "dtab_sb", words_of(dtab_words))
        slots_a = load([P, J // 16], U16, "slots_a", offs2, lists)
        gain_sb = load([P, PLACES], F32, "gain_sb", gain.rearrange("(p t) o -> p (t o)", t=PLACES))
        rs_sb = load([P, PLACES], F32, "rs_sb", rs.rearrange("(p t) o -> p (t o)", t=PLACES))
        slots_b = load([P, J // 16], U16, "slots_b", offs3, lists)
        ground_sb = [load([P, U], F32, "ground%d" % t, by_place(ground)[:, t, :]) for t in range(PLACES)]
        wor_raw = load([P, PLACES, F], F32, "wor_raw", by_place(wor))
        res_sb = load([P, PLACES, U], F32, "res_sb", by_place(res))

        def deal(copy, dealt, raw, m0, m1):
            copy(dealt[:, :, m0:m1, :].rearrange("p t m j -> p m t j"),
                 raw[:].rearrange("p j (m t) -> p m t j", t=PLACES)[:, m0:m1, :, :])

        def gather_words(words, name):
            codes = keep.tile([P, J], U32, name=name, align_bytes=64)
            nc.vector.tensor_copy(codes[:], words[:].bitcast(U32).indirect(columns[:]))
            return codes

        blocks = [slice(c0, c0 + P) for c0 in range(0, U, P)]

        w1_dealt = keep.tile([P, PLACES, P, PLACES], BF16, align_bytes=64)
        deal(nc.vector.tensor_copy, w1_dealt, w1_raw, 0, W1_ON_VECTOR)
        deal(nc.scalar.copy, w1_dealt, w1_raw, W1_ON_VECTOR, P)
        w1_codes = keep.tile([P, R], U32, align_bytes=64)
        w1_scales = keep.tile([P, R], U8, align_bytes=64)
        for t in range(PLACES):
            nc.vector.quantize_mx(out=w1_codes[:, blocks[t]].bitcast(FP8X4), scales=w1_scales[:, blocks[t]],
                                  in_=w1_dealt[:, t, :, :].rearrange("p m j -> p (m j)"))
        tab_codes = gather_words(tab_sb, "tab_codes")

        page_a = [zeroed([P, U], F32, name) for name in ("dtab_rows", "w1_raw", "page_a2", "w1_dealt")]
        page_b = [zeroed([P, U], F32, "tab_rows", nc.gpsimd)]
        page_b.extend(zeroed([P, U], F32, name) for name in ("picked", "page_b2", "tab_sb"))

        def first_layer(t, codes, scales, name):
            bank = psum.tile([P, J], F32, name="first_bank")
            nc.tensor.matmul_mx(out=bank[:], lhsT=w1_codes[:, blocks[t]].bitcast(FP8X4), lhsT_scale=w1_scales[:, blocks[t]],
                                rhs=codes[:].bitcast(FP8X4), rhs_scale=scales, start=True, stop=True)
            staged = keep.tile([P, 2, J], F32, name=name, align_bytes=64)
            nc.scalar.activation(staged[:, 0, :], bank[:], ACT.Copy, scale=gain_sb[:, t:t + 1])
            nc.scalar.copy(staged[:, 1, :], bank[:])
            return staged

        def put_on_pages(t, staged):
            nc.vector.tensor_copy(page_a[t][:].indirect(slots_a[:]), staged[:, 0, :])
            nc.vector.tensor_copy(page_b[t][:].indirect(slots_b[:]), staged[:, 1, :])

        def turned_sum(x, y):
            bank = turn.tile([P, U], F32, name="sum_bank")
            for us in blocks:
                nc.tensor.matmul(bank[:, us], lhsT=x[:, us], rhs=ident[:], is_transpose=True, start=True, stop=False)
                nc.tensor.matmul(bank[:, us], lhsT=y[:, us], rhs=ident[:], is_transpose=True, start=False, stop=True)
            return bank

        def back_bank(shape):
            return turn.tile(shape, F32, name="back_bank", bufs=3)

        for t in range(PLACES):
            put_on_pages(t, first_layer(t, tab_codes, listed_scales[:, 0:J], "forward%d" % t))
        dtab_codes = gather_words(dtab_sb, "dtab_codes")

        scaled_tanh = keep.tile([P, PLACES, U], F32)
        second_factor = keep.tile([P, 2, U], F32)
        slope = keep.tile([P, PLACES, U], F32)
        neg_rs = keep.tile([P, PLACES], F32)
        nc.scalar.activation(neg_rs[:], rs_sb[:], ACT.Copy, scale=-1.0)
        damping = []
        for t in range(PLACES):
            tanh_turned = keep.tile([P, U], F32, name="tanh_turned%d" % t, align_bytes=64)
            nc.scalar.activation(tanh_turned[:], turned_sum(ground_sb[t], page_a[t])[:], ACT.Tanh)
            tanh_bank = back_bank([P, U])
            for us in blocks:
                nc.tensor.transpose(tanh_bank[:, us], tanh_turned[:, us], ident[:])
            damping.append(keep.tile([P, U], F32, name="damping%d" % t, align_bytes=64))
            nc.scalar.activation(damping[t][:], tanh_bank[:], ACT.Square)
            nc.scalar.activation(damping[t][:], damping[t][:], ACT.Identity, scale=neg_rs[:, t:t + 1], bias=rs_sb[:, t:t + 1])
            if t < LAST:
                nc.scalar.activation(scaled_tanh[:, t, :], tanh_bank[:], ACT.Copy, scale=rs_sb[:, t:t + 1])
            nc.gpsimd.tensor_tensor(second_factor[:, t % 2, :], page_b[t][:], ground_sb[t][:], ALU.add)
            nc.gpsimd.tensor_tensor(slope[:, t, :], second_factor[:, t % 2, :], damping[t][:], ALU.mult)

        tangents = [first_layer(t, dtab_codes, listed_scales[:, J:2 * J], "tangent%d" % t) for t in range(PLACES)]

        wor_dealt = keep.tile([P, PLACES, P, PLACES], BF16, name="tanh_turned%d" % LAST, align_bytes=64)
        for m0 in range(0, P, WOR_PIECE):
            deal(nc.scalar.copy, wor_dealt, wor_raw, m0, m0 + WOR_PIECE)

        term_a = [second_factor[:, 0, :]] + [slope[:, t, :] for t in range(LAST)]
        term_b = [damping[2][:], scaled_tanh[:, 0, :], scaled_tanh[:, 1, :]]
        fo_turned = [damping[0][:], scaled_tanh[:, LAST, :]]
        for t in range(PLACES):
            put_on_pages(t, tangents[t])
            nc.gpsimd.tensor_tensor(term_a[t], page_a[t][:], slope[:, t, :], ALU.mult)
            if t < LAST:
                nc.gpsimd.tensor_tensor(term_b[t], page_b[t][:], scaled_tanh[:, t, :], ALU.mult)
            if t < len(fo_turned):
                nc.scalar.copy(fo_turned[t], turned_sum(term_a[t], term_b[t])[:])

        fo_rounded = keep.tile([P, U, PLACES], BF16, align_bytes=64)
        for half in range(2):
            both = back_bank([P, 2, U // 2])
            for b in range(2):
                for t in (1, 0):
                    nc.tensor.transpose(both[:, t, blocks[b]], fo_turned[t][:, blocks[2 * half + b]], ident[:])
            nc.scalar.copy(fo_rounded[:, half * (U // 2):(half + 1) * (U // 2), 0:2], by_column(both[:]))

        nc.vector.scalar_tensor_tensor(scaled_tanh[:, LAST, :], page_b[LAST][:], rs_sb[:, LAST:LAST + 1], tanh_bank[:],
                                       ALU.mult, ALU.mult)
        wor_codes = keep.tile([P, F], U32, name="damping0", align_bytes=64)
        wor_scales = keep.tile([P, F], U8, align_bytes=64)
        nc.vector.quantize_mx(out=wor_codes[:].bitcast(FP8X4), scales=wor_scales[:],
                              in_=wor_dealt[:].rearrange("p t m j -> p (t m j)"))

        fo_codes = keep.tile([P, U], U32, align_bytes=64)
        fo_scales = keep.tile([P, U], U8, align_bytes=64)
        y_codes = keep.tile([P, U], U32, align_bytes=64)
        y_scales = keep.tile([P, U], U8, align_bytes=64)
        y_rounded = keep.tile([P, U, PLACES], BF16, align_bytes=64)
        products = []
        for c, us in enumerate(blocks):
            nc.vector.tensor_tensor(fo_rounded[:, us, 2:4], by_column(slope[:, 1:3, us]), by_column(scaled_tanh[:, 1:4:2, us]),
                                    ALU.add)
            nc.vector.quantize_mx(out=fo_codes[:, us].bitcast(FP8X4), scales=fo_scales[:, us],
                                  in_=fo_rounded[:, us, :].rearrange("p u t -> p (u t)"))
            yo = psum.tile([P, PLACES, P], F32, name="first_bank" if c == len(blocks) - 1 else "last_bank%d" % c)
            for t in range(PLACES):
                nc.tensor.matmul_mx(out=yo[:, t, :], lhsT=wor_codes[:, blocks[t]].bitcast(FP8X4), lhsT_scale=wor_scales[:, blocks[t]],
                                    rhs=fo_codes[:, us].bitcast(FP8X4), rhs_scale=fo_scales[:, us], start=True, stop=True)
            products.append(yo)
        for c, (us, yo) in enumerate(zip(blocks, products)):
            y = keep.tile([P, PLACES, P], F32, name="y%d" % c)
            nc.vector.tensor_tensor(y[:], yo[:], res_sb[:, :, us], ALU.add)
            nc.sync.dma_start(by_place(out_0)[:, :, us], y[:])
            copy = nc.vector.tensor_copy if c == len(blocks) - 1 else nc.scalar.copy
            copy(y_rounded[:, us, :].rearrange("p (g i) t -> p g t i", i=4), y[:].rearrange("p t (g i) -> p g t i", i=4))
            nc.vector.quantize_mx(out=y_codes[:, us].bitcast(FP8X4), scales=y_scales[:, us],
                                  in_=y_rounded[:, us, :].rearrange("p u t -> p (u t)"))

        for us in (slice(0, U - P), blocks[-1]):
            nc.sync.dma_start(words_of(out_1)[:, us], y_codes[:, us].bitcast(I32))
        for q in range(QUADRANTS):
            queue = nc.scalar if q % 2 else nc.sync
            queue.dma_start(out_2[0, 4 * q:4 * q + 4, :].bitcast(I32), y_scales[32 * q:32 * q + 4, :].bitcast(I32))
